import numpy as np
import ml_dtypes


def mxq(x, axis, fmt="e4m3"):
    dtype, down = {"e4m3": (ml_dtypes.float8_e4m3fn, 7), "e5m2": (ml_dtypes.float8_e5m2, 14)}[fmt]
    v = np.moveaxis(np.asarray(x, np.float32).astype(ml_dtypes.bfloat16).astype(np.float64), axis, -1)
    blocks = v.reshape(v.shape[:-1] + (-1, 32))
    amax = np.abs(blocks).max(-1, keepdims=True)
    byte = np.maximum(np.where(amax > 0, np.frexp(amax)[1] - 1 + 127, 0) - down, 1)
    scale = np.exp2(byte - 127.0)
    codes = (blocks / scale).astype(np.float32).astype(dtype).astype(np.float64)
    return np.moveaxis((codes * scale).reshape(v.shape), -1, axis)


WIDE = False


def mx_kscale(k):
    if not WIDE:
        return np.ones(k)
    levels = np.array([10, -10, 5, -5, 0])
    if k % 512:
        return np.exp2(np.random.permutation(np.resize(levels, k // 32))).repeat(32)
    a = np.empty((k // 512, 16))
    for p in range(k // 512):
        a[p, :8] = np.random.permutation(np.resize(levels, 8))
        for g in range(8):
            far = levels[np.abs(levels - a[p, g]) >= 10]
            a[p, g + 8] = far[np.random.randint(len(far))]
    return np.exp2(a.ravel()).repeat(32)


def f64(x):
    return np.asarray(x).astype(np.float64)


def striped(idx):
    return np.tile(idx.reshape(-1, 16).T, (8, 1)).astype(np.uint16)


def unstriped(offs):
    return offs[:16].T.reshape(-1).astype(np.int64)


def striped8(idx):
    return np.concatenate([x.reshape(-1, 16).T for x in idx]).astype(np.uint16)


def runs(offs, k):
    lists = np.stack([offs[16 * r : 16 * r + 16].T.reshape(-1) for r in range(8)]).astype(np.int64)
    return lists[np.arange(k) % 512 // 64]


def pack_weight(w):
    k, n = w.shape
    w = f64(np.asarray(w, np.float32).astype(ml_dtypes.bfloat16)).reshape(k // 32, 32, n)
    amax = np.abs(w).max(1)
    byte = np.clip(np.where(amax > 0, np.frexp(amax)[1] - 1 + 127 - 7, 1), 1, 254)
    scaled = (w * np.exp2(127.0 - byte)[:, None, :]).reshape(k, n).astype(np.float32)
    words = np.ascontiguousarray(scaled.reshape(k // 512, 128, 4, n).transpose(0, 1, 3, 2)).astype(ml_dtypes.float8_e4m3fn).view(np.uint8)
    return words, np.ascontiguousarray(byte.astype(np.uint8).reshape(k // 512, 16, n))


def unpack_weight(words, scales):
    g, p, n, _ = words.shape
    vals = np.ascontiguousarray(words).view(ml_dtypes.float8_e4m3fn).astype(np.float64) * np.repeat(np.exp2(scales.astype(np.float64) - 127.0), 8, axis=1)[..., None]
    return vals.transpose(0, 1, 3, 2).reshape(g * 512, n)


def sigmoid(v):
    return 1.0 / (1.0 + np.exp(-np.maximum(v, -700.0)))


K, T, S, V, N, H = 512, 2048, 512, 256, 512, 512


def setup_inputs():
    n = np.random.standard_normal
    s = mx_kscale(K)[:, None]
    u = mx_kscale(S)
    packed_xT = pack_weight(n((K, T)) * s)
    return {
        "x_words": packed_xT[0],
        "x_scales": packed_xT[1],
        "wa": (n((K, H)) / np.sqrt(K) / s).astype(np.float32),
        "gt": (np.random.uniform(0.5, 1.5, (S, 1)) * u[:, None]).astype(np.float32),
        "w1": (n((S, N)) / np.sqrt(S) / u[:, None]).astype(np.float32),
        "offs": striped(np.random.permutation(T)[:S]),
        "order": striped8(np.stack([np.random.permutation(H) for _ in range(8)])),
    }


def reference(x_words, x_scales, wa, gt, w1, offs, order):
    xq = unpack_weight(x_words, x_scales)[:, unstriped(offs)]
    y = xq.T @ mxq(f64(wa), 0, "e4m3")
    o = y[np.arange(S)[:, None], runs(order, S)]
    mx = o.reshape(S, V, 2).max(axis=2)
    mn = o.reshape(S, V, 2).min(axis=2)
    z = f64(gt) * (mx * sigmoid(mn))
    return mxq(f64(w1), 0, "e4m3").T @ mxq(z, 0, "e4m3")

@@ -1,0 +1,169 @@
+from contextlib import ExitStack
+
+import concourse.mybir as mybir
+
+F32 = mybir.dt.float32
+BF16 = mybir.dt.bfloat16
+I32 = mybir.dt.int32
+U32 = mybir.dt.uint32
+U16 = mybir.dt.uint16
+U8 = mybir.dt.uint8
+FP8X4 = mybir.dt.float8_e4m3fn_x4
+ALU = mybir.AluOpType
+ACT = mybir.ActivationFunctionType
+
+P = 128
+PACK = 4
+K, T, S, V, N, H = 512, 2048, 512, 256, 512, 512
+FLOPS = 2 * K * S * H + 2 * S * N * V
+W_CHUNK = 128
+PAIR_CHUNKS = [(0, 128), (128, 64), (192, 64)]
+
+
+def tile_picked_featwin_none_p_kernel(tc, x_words, x_scales, wa, gt, w1, offs, order, out):
+    nc = tc.nc
+    with ExitStack() as ctx:
+        keep = ctx.enter_context(tc.tile_pool(name="keep", bufs=1))
+        psum = ctx.enter_context(tc.psum_pool(name="psum", bufs=1))
+
+        offs_sb = keep.tile([P, S // 16], U16, name="offs_sb")
+        order_sb = keep.tile([P, H // 16], U16, name="order_sb")
+        words_all = keep.tile([P, T], I32, name="words_all", align_bytes=64)
+        scales_all = keep.tile([P, T], U8, name="scales_all", align_bytes=64)
+        gate = keep.tile([P, PACK], F32, name="gate")
+        warm = keep.tile([P, 8], F32, name="warm", tag="warm")
+        warm_out = keep.tile([P, 8], F32, name="warm_out")
+
+        n_chunks = H // W_CHUNK
+        wa_rows = wa.rearrange("(p j) h -> p j h", j=PACK)
+        w1_rows = w1.rearrange("(p j) m -> p j m", j=PACK)
+        wa_first = keep.tile([P, PACK, W_CHUNK], F32, name="wa_first")
+
+        nc.sync.dma_start(offs_sb[:], offs)
+        nc.sync.dma_start(order_sb[:], order)
+        nc.sync.dma_start(wa_first[:], wa_rows[:, :, 0:W_CHUNK])
+        scale_words = scales_all[:].bitcast(I32)
+        nc.vector.memset(scale_words[:, 0 : T // 8], 0)
+        nc.gpsimd.memset(scale_words[:, T // 8 : T // 4], 0)
+        nc.vector.memset(warm[:], 0.0)
+        nc.gpsimd.dma_start(gate[:], gt.rearrange("(p j) o -> p (j o)", j=PACK))
+        for q in range(4):
+            nc.sync.dma_start(scales_all[32 * q : 32 * q + 4, :].bitcast(I32), x_scales[0, 4 * q : 4 * q + 4, :].bitcast(I32))
+        nc.scalar.activation(warm_out[:], warm[:], ACT.Sigmoid)
+        nc.sync.dma_start(words_all[:], x_words[0].rearrange("p n r -> p (n r)").bitcast(I32))
+
+        later = keep.tile([P, (2 * n_chunks - 1) * PACK * W_CHUNK], F32, name="later", tag="warm")
+        unit = PACK * W_CHUNK
+        wa_raw = [wa_first[:]] + [later[:, c * unit : (c + 1) * unit].rearrange("p (j h) -> p j h", j=PACK) for c in range(n_chunks - 1)]
+        w1_raw = [later[:, (3 + 2 * c) * unit : (5 + 2 * c) * unit].rearrange("p (j h) -> p j h", j=PACK) for c in range(2)]
+        for c in range(1, n_chunks):
+            nc.sync.dma_start(wa_raw[c], wa_rows[:, :, c * W_CHUNK : (c + 1) * W_CHUNK])
+        for c in range(2):
+            nc.sync.dma_start(w1_raw[c], w1_rows[:, :, 2 * c * W_CHUNK : 2 * (c + 1) * W_CHUNK])
+
+        scales_picked = keep.tile([P, S], U8, name="scales_picked", align_bytes=64)
+        x_scale = keep.tile([P, PACK, P], U8, name="x_scale", align_bytes=64)
+        x_codes = keep.tile([P, PACK, P], U32, name="x_codes", align_bytes=64)
+        nc.vector.tensor_copy(scales_picked[:], scales_all[:].indirect(offs_sb[:]))
+        nc.vector.tensor_copy(x_scale[:], scales_picked[:].rearrange("p (m j) -> p j m", j=PACK))
+        nc.vector.tensor_copy(x_codes[:].rearrange("p j m -> p m j"), words_all[:].bitcast(U32).indirect(offs_sb[:]))
+
+        wa_codes = keep.tile([P, H], U32, name="wa_codes", tag="wa_codes", align_bytes=64)
+        wa_scale = keep.tile([P, H], U8, name="wa_scale", align_bytes=64)
+        wa_bf = [keep.tile([P, W_CHUNK, PACK], BF16, name="wa_bf%d" % c, align_bytes=64) for c in range(n_chunks)]
+
+        def interleave(on_scalar, dst, src):
+            if on_scalar:
+                nc.scalar.copy(dst, src.rearrange("p j c -> p c j"))
+            else:
+                nc.vector.tensor_copy(dst, src.rearrange("p j c -> p c j"))
+
+        def quantize(codes, scale, grouped):
+            nc.vector.quantize_mx(out=codes.bitcast(FP8X4), scales=scale, in_=grouped.rearrange("p c j -> p (c j)"))
+
+        for c in range(n_chunks):
+            cols = slice(c * W_CHUNK, (c + 1) * W_CHUNK)
+            interleave(c in [0,1,2], wa_bf[c][:], wa_raw[c])
+            quantize(wa_codes[:, cols], wa_scale[:, cols], wa_bf[c][:])
+
+        y = [keep.tile([P, H], F32, name="y%d" % j) for j in range(PACK)]
+        early = [psum.tile([P, 512], F32, name="bank%d" % j, tag="bank%d" % j) for j in range(PACK)]
+        late = [psum.tile([P, 512], F32, name="bank%d" % (PACK + j), tag="bank%d" % (PACK + j)) for j in range(PACK)]
+
+        def first_product(dst, j, cols):
+            nc.tensor.matmul_mx(out=dst, lhsT=x_codes[:, j, :].bitcast(FP8X4), lhsT_scale=x_scale[:, j, :],
+                                rhs=wa_codes[:, cols].bitcast(FP8X4), rhs_scale=wa_scale[:, cols], start=True, stop=True)
+
+        for j in range(PACK):
+            first_product(early[j][:, 0:256], j, slice(0, 256))
+            first_product(late[j][:, 0:256], j, slice(256, 512))
+        for j in range(PACK):
+            nc.scalar.copy(y[j][:, 0:256], early[j][:, 0:256])
+            if j == 0:
+                nc.vector.tensor_copy(y[j][:, 256:512], late[j][:, 0:256])
+            else:
+                nc.scalar.copy(y[j][:, 256:512], late[j][:, 0:256])
+
+        w1_codes = keep.tile([P, N], U32, name="w1_codes", align_bytes=64)
+        w1_scale = keep.tile([P, N], U8, name="w1_scale", align_bytes=64)
+        w1_bf = keep.tile([P, N, PACK], BF16, name="w1_bf", tag="wa_codes", align_bytes=64)
+
+        def group_w1(h):
+            for c in (2 * h, 2 * h + 1):
+                half = slice((c % 2) * W_CHUNK, (c % 2 + 1) * W_CHUNK)
+                interleave(True, w1_bf[:, c * W_CHUNK : (c + 1) * W_CHUNK, :], w1_raw[h][:, :, half])
+
+        group_w1(0)
+
+        out_rows = out.rearrange("(b p) v -> p b v", p=P)
+        nch = len(PAIR_CHUNKS)
+        lined = {}
+        small = [keep.tile([P, PACK, w], F32, name="small%d" % c) for c, (v0, w) in enumerate(PAIR_CHUNKS)]
+        large = [keep.tile([P, PACK, w], F32, name="large%d" % c) for c, (v0, w) in enumerate(PAIR_CHUNKS)]
+        sig = [keep.tile([P, PACK, w], F32, name="sig%d" % c) for c, (v0, w) in enumerate(PAIR_CHUNKS)]
+        z_rows = [keep.tile([P, PACK, w], BF16, name="z_rows%d" % c) for c, (v0, w) in enumerate(PAIR_CHUNKS)]
+        z_bf = [keep.tile([P, w, PACK], BF16, name="z_bf%d" % c, align_bytes=64) for c, (v0, w) in enumerate(PAIR_CHUNKS)]
+
+        def fetch(c):
+            v0, w = PAIR_CHUNKS[c]
+            lined.setdefault(c, keep.tile([P, PACK, 2 * w], F32, name="lined%d" % c, tag="lined"))
+            for j in range(PACK):
+                nc.vector.tensor_copy(lined[c][:, j, :], y[j][:].indirect(order_sb[:, v0 // 8 : (v0 + w) // 8]))
+
+        def compete(c):
+            pairs = lined[c][:].rearrange("p j (v e) -> p j v e", e=2)
+            nc.vector.tensor_tensor(small[c][:], pairs[:, :, :, 0], pairs[:, :, :, 1], ALU.min)
+            nc.scalar.activation(sig[c][:], small[c][:], ACT.Sigmoid)
+            nc.vector.tensor_tensor(large[c][:], pairs[:, :, :, 0], pairs[:, :, :, 1], ALU.max)
+
+        def weigh(c):
+            for j in range(PACK):
+                nc.vector.scalar_tensor_tensor(z_rows[c][:, j, :], large[c][:, j, :], gate[:, j : j + 1], sig[c][:, j, :], ALU.mult, ALU.mult)
+            interleave(not (c == len(PAIR_CHUNKS) - 1), z_bf[c][:], z_rows[c][:])
+
+        def mix(c):
+            v0, w = PAIR_CHUNKS[c]
+            z_codes = keep.tile([P, w], U32, name="z_codes%d" % c, align_bytes=64)
+            z_scale = keep.tile([P, w], U8, name="z_scale%d" % c, align_bytes=64)
+            quantize(z_codes[:], z_scale[:], z_bf[c][:])
+            acc = psum.tile([P, 512], F32, name="acc%d" % c, tag="bank%d" % c)
+            for b in range(N // P):
+                cols = slice(b * P, (b + 1) * P)
+                nc.tensor.matmul_mx(out=acc[:, b * w : (b + 1) * w], lhsT=w1_codes[:, cols].bitcast(FP8X4), lhsT_scale=w1_scale[:, cols],
+                                    rhs=z_codes[:].bitcast(FP8X4), rhs_scale=z_scale[:], start=True, stop=True)
+            res = keep.tile([P, N // P, w], F32, name="res%d" % c)
+            nc.scalar.copy(res[:].rearrange("p b v -> p (b v)"), acc[:, 0 : (N // P) * w])
+            nc.sync.dma_start(out_rows[:, :, v0 : v0 + w], res[:])
+
+        fetch(0)
+        compete(0)
+        group_w1(1)
+        for c in range(1, nch):
+            fetch(c)
+            weigh(c - 1)
+            compete(c)
+            if c == 1:
+                quantize(w1_codes[:], w1_scale[:], w1_bf[:])
+            mix(c - 1)
+        weigh(nch - 1)
+        mix(nch - 1)

@@ -30,7 +30,6 @@ def tile_picked_featwin_none_p_kernel(tc, x_words, x_scales, wa, gt, w1, offs, o
         order_sb = keep.tile([P, H // 16], U16, name="order_sb")
         words_all = keep.tile([P, T], I32, name="words_all", align_bytes=64)
         scales_all = keep.tile([P, T], U8, name="scales_all", align_bytes=64)
-        gate = keep.tile([P, PACK], F32, name="gate")
         warm = keep.tile([P, 8], F32, name="warm", tag="warm")
         warm_out = keep.tile([P, 8], F32, name="warm_out")
 
@@ -39,25 +38,26 @@ def tile_picked_featwin_none_p_kernel(tc, x_words, x_scales, wa, gt, w1, offs, o
         w1_rows = w1.rearrange("(p j) m -> p j m", j=PACK)
         wa_first = keep.tile([P, PACK, W_CHUNK], F32, name="wa_first")
 
+        nc.sync.dma_start(wa_first[:], wa_rows[:, :, 0:W_CHUNK])
         nc.sync.dma_start(offs_sb[:], offs)
         nc.sync.dma_start(order_sb[:], order)
-        nc.sync.dma_start(wa_first[:], wa_rows[:, :, 0:W_CHUNK])
         scale_words = scales_all[:].bitcast(I32)
         nc.vector.memset(scale_words[:, 0 : T // 8], 0)
         nc.gpsimd.memset(scale_words[:, T // 8 : T // 4], 0)
         nc.vector.memset(warm[:], 0.0)
-        nc.gpsimd.dma_start(gate[:], gt.rearrange("(p j) o -> p (j o)", j=PACK))
-        for q in range(4):
-            nc.sync.dma_start(scales_all[32 * q : 32 * q + 4, :].bitcast(I32), x_scales[0, 4 * q : 4 * q + 4, :].bitcast(I32))
+        for r in range(4):
+            nc.sync.dma_start(scale_words[r:P:32, :], x_scales[0, r:16:4, :].bitcast(I32))
         nc.scalar.activation(warm_out[:], warm[:], ACT.Sigmoid)
         nc.sync.dma_start(words_all[:], x_words[0].rearrange("p n r -> p (n r)").bitcast(I32))
 
-        later = keep.tile([P, (2 * n_chunks - 1) * PACK * W_CHUNK], F32, name="later", tag="warm")
+        later = keep.tile([P, (2 * n_chunks - 1) * PACK * W_CHUNK + PACK], F32, name="later", tag="warm")
         unit = PACK * W_CHUNK
         wa_raw = [wa_first[:]] + [later[:, c * unit : (c + 1) * unit].rearrange("p (j h) -> p j h", j=PACK) for c in range(n_chunks - 1)]
         w1_raw = [later[:, (3 + 2 * c) * unit : (5 + 2 * c) * unit].rearrange("p (j h) -> p j h", j=PACK) for c in range(2)]
         for c in range(1, n_chunks):
             nc.sync.dma_start(wa_raw[c], wa_rows[:, :, c * W_CHUNK : (c + 1) * W_CHUNK])
+        gate = later[:, 7 * unit : 7 * unit + PACK]
+        nc.sync.dma_start(gate, gt.rearrange("(p j) o -> p (j o)", j=PACK))
         for c in range(2):
             nc.sync.dma_start(w1_raw[c], w1_rows[:, :, 2 * c * W_CHUNK : 2 * (c + 1) * W_CHUNK])
 
@@ -83,26 +83,24 @@ def tile_picked_featwin_none_p_kernel(tc, x_words, x_scales, wa, gt, w1, offs, o
 
         for c in range(n_chunks):
             cols = slice(c * W_CHUNK, (c + 1) * W_CHUNK)
-            interleave(c in [0,1,2], wa_bf[c][:], wa_raw[c])
+            if c < n_chunks - 1:
+                interleave(True, wa_bf[c][:], wa_raw[c])
+            else:
+                interleave(True, wa_bf[c][:, 0:48, :], wa_raw[c][:, :, 0:48])
+                interleave(False, wa_bf[c][:, 48:128, :], wa_raw[c][:, :, 48:128])
             quantize(wa_codes[:, cols], wa_scale[:, cols], wa_bf[c][:])
 
         y = [keep.tile([P, H], F32, name="y%d" % j) for j in range(PACK)]
-        early = [psum.tile([P, 512], F32, name="bank%d" % j, tag="bank%d" % j) for j in range(PACK)]
-        late = [psum.tile([P, 512], F32, name="bank%d" % (PACK + j), tag="bank%d" % (PACK + j)) for j in range(PACK)]
+        parts = [(0, slice(0, 256)), (0, slice(256, 384)), (0, slice(384, 512))] + [(j, slice(0, H)) for j in range(1, PACK)]
+        banks = [psum.tile([P, 512], F32, name="bank%d" % n, tag="bank%d" % n) for n in range(len(parts))]
 
         def first_product(dst, j, cols):
             nc.tensor.matmul_mx(out=dst, lhsT=x_codes[:, j, :].bitcast(FP8X4), lhsT_scale=x_scale[:, j, :],
                                 rhs=wa_codes[:, cols].bitcast(FP8X4), rhs_scale=wa_scale[:, cols], start=True, stop=True)
 
-        for j in range(PACK):
-            first_product(early[j][:, 0:256], j, slice(0, 256))
-            first_product(late[j][:, 0:256], j, slice(256, 512))
-        for j in range(PACK):
-            nc.scalar.copy(y[j][:, 0:256], early[j][:, 0:256])
-            if j == 0:
-                nc.vector.tensor_copy(y[j][:, 256:512], late[j][:, 0:256])
-            else:
-                nc.scalar.copy(y[j][:, 256:512], late[j][:, 0:256])
+        for n, (j, cols) in enumerate(parts):
+            first_product(banks[n][:, cols], j, cols)
+            nc.scalar.copy(y[j][:, cols], banks[n][:, cols])
 
         w1_codes = keep.tile([P, N], U32, name="w1_codes", align_bytes=64)
         w1_scale = keep.tile([P, N], U8, name="w1_scale", align_bytes=64)
@@ -116,54 +114,76 @@ def tile_picked_featwin_none_p_kernel(tc, x_words, x_scales, wa, gt, w1, offs, o
         group_w1(0)
 
         out_rows = out.rearrange("(b p) v -> p b v", p=P)
-        nch = len(PAIR_CHUNKS)
-        lined = {}
-        small = [keep.tile([P, PACK, w], F32, name="small%d" % c) for c, (v0, w) in enumerate(PAIR_CHUNKS)]
-        large = [keep.tile([P, PACK, w], F32, name="large%d" % c) for c, (v0, w) in enumerate(PAIR_CHUNKS)]
-        sig = [keep.tile([P, PACK, w], F32, name="sig%d" % c) for c, (v0, w) in enumerate(PAIR_CHUNKS)]
-        z_rows = [keep.tile([P, PACK, w], BF16, name="z_rows%d" % c) for c, (v0, w) in enumerate(PAIR_CHUNKS)]
-        z_bf = [keep.tile([P, w, PACK], BF16, name="z_bf%d" % c, align_bytes=64) for c, (v0, w) in enumerate(PAIR_CHUNKS)]
+        w = V // 2
+        lined = keep.tile([P, PACK, 2 * w], F32, name="lined")
+        pairs = lined[:].rearrange("p j (v e) -> p j v e", e=2)
+        small = [keep.tile([P, PACK, w], F32, name="small%d" % c) for c in range(2)]
+        large = [keep.tile([P, PACK, w], F32, name="large%d" % c) for c in range(2)]
+        sig = [keep.tile([P, PACK, w], F32, name="sig%d" % c) for c in range(2)]
+        z_rows = [keep.tile([P, PACK, w], BF16, name="z_rows%d" % c) for c in range(2)]
+        z_bf = [keep.tile([P, w, PACK], BF16, name="z_bf%d" % c, align_bytes=64) for c in range(2)]
+        z_codes = [keep.tile([P, w], U32, name="z_codes%d" % c, align_bytes=64) for c in range(2)]
+        z_scale = [keep.tile([P, w], U8, name="z_scale%d" % c, align_bytes=64) for c in range(2)]
+        res = [keep.tile([P, N // P, w], F32, name="res%d" % c) for c in range(2)]
 
-        def fetch(c):
-            v0, w = PAIR_CHUNKS[c]
-            lined.setdefault(c, keep.tile([P, PACK, 2 * w], F32, name="lined%d" % c, tag="lined"))
-            for j in range(PACK):
-                nc.vector.tensor_copy(lined[c][:, j, :], y[j][:].indirect(order_sb[:, v0 // 8 : (v0 + w) // 8]))
+        def fetch(c, j):
+            nc.vector.tensor_copy(lined[:, j, :], y[j][:].indirect(order_sb[:, c * w // 8 : (c + 1) * w // 8]))
 
-        def compete(c):
-            pairs = lined[c][:].rearrange("p j (v e) -> p j v e", e=2)
-            nc.vector.tensor_tensor(small[c][:], pairs[:, :, :, 0], pairs[:, :, :, 1], ALU.min)
-            nc.scalar.activation(sig[c][:], small[c][:], ACT.Sigmoid)
-            nc.vector.tensor_tensor(large[c][:], pairs[:, :, :, 0], pairs[:, :, :, 1], ALU.max)
+        def smaller(c, h):
+            js = slice(2 * h, 2 * h + 2)
+            nc.vector.tensor_tensor(small[c][:, js, :], pairs[:, js, :, 0], pairs[:, js, :, 1], ALU.min)
+            nc.scalar.activation(sig[c][:, js, :], small[c][:, js, :], ACT.Sigmoid)
 
-        def weigh(c):
-            for j in range(PACK):
-                nc.vector.scalar_tensor_tensor(z_rows[c][:, j, :], large[c][:, j, :], gate[:, j : j + 1], sig[c][:, j, :], ALU.mult, ALU.mult)
-            interleave(not (c == len(PAIR_CHUNKS) - 1), z_bf[c][:], z_rows[c][:])
+        def larger(c, h):
+            js = slice(2 * h, 2 * h + 2)
+            nc.vector.tensor_tensor(large[c][:, js, :], pairs[:, js, :, 0], pairs[:, js, :, 1], ALU.max)
 
-        def mix(c):
-            v0, w = PAIR_CHUNKS[c]
-            z_codes = keep.tile([P, w], U32, name="z_codes%d" % c, align_bytes=64)
-            z_scale = keep.tile([P, w], U8, name="z_scale%d" % c, align_bytes=64)
-            quantize(z_codes[:], z_scale[:], z_bf[c][:])
-            acc = psum.tile([P, 512], F32, name="acc%d" % c, tag="bank%d" % c)
-            for b in range(N // P):
+        def weigh(c, j):
+            nc.vector.scalar_tensor_tensor(z_rows[c][:, j, :], large[c][:, j, :], gate[:, j : j + 1], sig[c][:, j, :], ALU.mult, ALU.mult)
+
+        def mix(c, bank, blocks, on_scalar):
+            acc = psum.tile([P, 512], F32, name="acc%d" % bank, tag="bank%d" % bank)
+            for i, b in enumerate(blocks):
                 cols = slice(b * P, (b + 1) * P)
-                nc.tensor.matmul_mx(out=acc[:, b * w : (b + 1) * w], lhsT=w1_codes[:, cols].bitcast(FP8X4), lhsT_scale=w1_scale[:, cols],
-                                    rhs=z_codes[:].bitcast(FP8X4), rhs_scale=z_scale[:], start=True, stop=True)
-            res = keep.tile([P, N // P, w], F32, name="res%d" % c)
-            nc.scalar.copy(res[:].rearrange("p b v -> p (b v)"), acc[:, 0 : (N // P) * w])
-            nc.sync.dma_start(out_rows[:, :, v0 : v0 + w], res[:])
+                nc.tensor.matmul_mx(out=acc[:, i * w : (i + 1) * w], lhsT=w1_codes[:, cols].bitcast(FP8X4), lhsT_scale=w1_scale[:, cols],
+                                    rhs=z_codes[c][:].bitcast(FP8X4), rhs_scale=z_scale[c][:], start=True, stop=True)
+            rows = res[c][:, blocks[0] : blocks[-1] + 1, :]
+            if on_scalar:
+                nc.scalar.copy(rows.rearrange("p b v -> p (b v)"), acc[:, 0 : len(blocks) * w])
+            else:
+                nc.vector.tensor_copy(rows.rearrange("p b v -> p (b v)"), acc[:, 0 : len(blocks) * w])
 
-        fetch(0)
-        compete(0)
+        def store(c, first, last):
+            nc.sync.dma_start(out_rows[:, first:last, c * w : (c + 1) * w], res[c][:, first:last, :])
+
+        for j in range(PACK):
+            fetch(0, j)
+        for h in range(2):
+            smaller(0, h)
+            larger(0, h)
         group_w1(1)
-        for c in range(1, nch):
-            fetch(c)
-            weigh(c - 1)
-            compete(c)
-            if c == 1:
-                quantize(w1_codes[:], w1_scale[:], w1_bf[:])
-            mix(c - 1)
-        weigh(nch - 1)
-        mix(nch - 1)
+        fetch(1, 0)
+        fetch(1, 1)
+        weigh(0, 0)
+        weigh(0, 1)
+        fetch(1, 2)
+        weigh(0, 2)
+        weigh(0, 3)
+        interleave(True, z_bf[0][:], z_rows[0][:])
+        fetch(1, 3)
+        quantize(w1_codes[:], w1_scale[:], w1_bf[:])
+        smaller(1, 0)
+        smaller(1, 1)
+        quantize(z_codes[0][:], z_scale[0][:], z_bf[0][:])
+        larger(1, 0)
+        larger(1, 1)
+        mix(0, 0, [0, 1, 2, 3], True)
+        store(0, 0, 4)
+        for j in range(PACK):
+            weigh(1, j)
+        interleave(False, z_bf[1][:], z_rows[1][:])
+        quantize(z_codes[1][:], z_scale[1][:], z_bf[1][:])
+        for b in range(N // P):
+            mix(1, 1 + b, [b], b % 2 == 0)
+            if b % 2 == 1:
+                store(1, b - 1, b + 1)

from contextlib import ExitStack

import concourse.mybir as mybir

F32 = mybir.dt.float32
BF16 = mybir.dt.bfloat16
I32 = mybir.dt.int32
U32 = mybir.dt.uint32
U16 = mybir.dt.uint16
U8 = mybir.dt.uint8
FP8X4 = mybir.dt.float8_e4m3fn_x4
ALU = mybir.AluOpType
ACT = mybir.ActivationFunctionType

P = 128
PACK = 4
K, T, S, V, N, H = 512, 2048, 512, 256, 512, 512
FLOPS = 2 * K * S * H + 2 * S * N * V
W_CHUNK = 128
PAIR_CHUNKS = [(0, 128), (128, 64), (192, 64)]


def tile_picked_featwin_none_p_kernel(tc, x_words, x_scales, wa, gt, w1, offs, order, out):
    nc = tc.nc
    with ExitStack() as ctx:
        keep = ctx.enter_context(tc.tile_pool(name="keep", bufs=1))
        psum = ctx.enter_context(tc.psum_pool(name="psum", bufs=1))

        offs_sb = keep.tile([P, S // 16], U16, name="offs_sb")
        order_sb = keep.tile([P, H // 16], U16, name="order_sb")
        words_all = keep.tile([P, T], I32, name="words_all", align_bytes=64)
        scales_all = keep.tile([P, T], U8, name="scales_all", align_bytes=64)
        warm = keep.tile([P, 8], F32, name="warm", tag="warm")
        warm_out = keep.tile([P, 8], F32, name="warm_out")

        n_chunks = H // W_CHUNK
        wa_rows = wa.rearrange("(p j) h -> p j h", j=PACK)
        w1_rows = w1.rearrange("(p j) m -> p j m", j=PACK)
        wa_first = keep.tile([P, PACK, W_CHUNK], F32, name="wa_first")

        nc.sync.dma_start(wa_first[:], wa_rows[:, :, 0:W_CHUNK])
        nc.sync.dma_start(offs_sb[:], offs)
        nc.sync.dma_start(order_sb[:], order)
        scale_words = scales_all[:].bitcast(I32)
        nc.vector.memset(scale_words[:, 0 : T // 8], 0)
        nc.gpsimd.memset(scale_words[:, T // 8 : T // 4], 0)
        nc.vector.memset(warm[:], 0.0)
        for r in range(4):
            nc.sync.dma_start(scale_words[r:P:32, :], x_scales[0, r:16:4, :].bitcast(I32))
        nc.scalar.activation(warm_out[:], warm[:], ACT.Sigmoid)
        nc.sync.dma_start(words_all[:], x_words[0].rearrange("p n r -> p (n r)").bitcast(I32))

        later = keep.tile([P, (2 * n_chunks - 1) * PACK * W_CHUNK + PACK], F32, name="later", tag="warm")
        unit = PACK * W_CHUNK
        wa_raw = [wa_first[:]] + [later[:, c * unit : (c + 1) * unit].rearrange("p (j h) -> p j h", j=PACK) for c in range(n_chunks - 1)]
        w1_raw = [later[:, (3 + 2 * c) * unit : (5 + 2 * c) * unit].rearrange("p (j h) -> p j h", j=PACK) for c in range(2)]
        for c in range(1, n_chunks):
            nc.sync.dma_start(wa_raw[c], wa_rows[:, :, c * W_CHUNK : (c + 1) * W_CHUNK])
        gate = later[:, 7 * unit : 7 * unit + PACK]
        nc.sync.dma_start(gate, gt.rearrange("(p j) o -> p (j o)", j=PACK))
        for c in range(2):
            nc.sync.dma_start(w1_raw[c], w1_rows[:, :, 2 * c * W_CHUNK : 2 * (c + 1) * W_CHUNK])

        scales_picked = keep.tile([P, S], U8, name="scales_picked", align_bytes=64)
        x_scale = keep.tile([P, PACK, P], U8, name="x_scale", align_bytes=64)
        x_codes = keep.tile([P, PACK, P], U32, name="x_codes", align_bytes=64)
        nc.vector.tensor_copy(scales_picked[:], scales_all[:].indirect(offs_sb[:]))
        nc.vector.tensor_copy(x_scale[:], scales_picked[:].rearrange("p (m j) -> p j m", j=PACK))
        nc.vector.tensor_copy(x_codes[:].rearrange("p j m -> p m j"), words_all[:].bitcast(U32).indirect(offs_sb[:]))

        wa_codes = keep.tile([P, H], U32, name="wa_codes", tag="wa_codes", align_bytes=64)
        wa_scale = keep.tile([P, H], U8, name="wa_scale", align_bytes=64)
        wa_bf = [keep.tile([P, W_CHUNK, PACK], BF16, name="wa_bf%d" % c, align_bytes=64) for c in range(n_chunks)]

        def interleave(on_scalar, dst, src):
            if on_scalar:
                nc.scalar.copy(dst, src.rearrange("p j c -> p c j"))
            else:
                nc.vector.tensor_copy(dst, src.rearrange("p j c -> p c j"))

        def quantize(codes, scale, grouped):
            nc.vector.quantize_mx(out=codes.bitcast(FP8X4), scales=scale, in_=grouped.rearrange("p c j -> p (c j)"))

        for c in range(n_chunks):
            cols = slice(c * W_CHUNK, (c + 1) * W_CHUNK)
            if c < n_chunks - 1:
                interleave(True, wa_bf[c][:], wa_raw[c])
            else:
                interleave(True, wa_bf[c][:, 0:48, :], wa_raw[c][:, :, 0:48])
                interleave(False, wa_bf[c][:, 48:128, :], wa_raw[c][:, :, 48:128])
            quantize(wa_codes[:, cols], wa_scale[:, cols], wa_bf[c][:])

        y = [keep.tile([P, H], F32, name="y%d" % j) for j in range(PACK)]
        parts = [(0, slice(0, 256)), (0, slice(256, 384)), (0, slice(384, 512))] + [(j, slice(0, H)) for j in range(1, PACK)]
        banks = [psum.tile([P, 512], F32, name="bank%d" % n, tag="bank%d" % n) for n in range(len(parts))]

        def first_product(dst, j, cols):
            nc.tensor.matmul_mx(out=dst, lhsT=x_codes[:, j, :].bitcast(FP8X4), lhsT_scale=x_scale[:, j, :],
                                rhs=wa_codes[:, cols].bitcast(FP8X4), rhs_scale=wa_scale[:, cols], start=True, stop=True)

        for n, (j, cols) in enumerate(parts):
            first_product(banks[n][:, cols], j, cols)
            nc.scalar.copy(y[j][:, cols], banks[n][:, cols])

        w1_codes = keep.tile([P, N], U32, name="w1_codes", align_bytes=64)
        w1_scale = keep.tile([P, N], U8, name="w1_scale", align_bytes=64)
        w1_bf = keep.tile([P, N, PACK], BF16, name="w1_bf", tag="wa_codes", align_bytes=64)

        def group_w1(h):
            for c in (2 * h, 2 * h + 1):
                half = slice((c % 2) * W_CHUNK, (c % 2 + 1) * W_CHUNK)
                interleave(True, w1_bf[:, c * W_CHUNK : (c + 1) * W_CHUNK, :], w1_raw[h][:, :, half])

        group_w1(0)

        out_rows = out.rearrange("(b p) v -> p b v", p=P)
        w = V // 2
        lined = keep.tile([P, PACK, 2 * w], F32, name="lined")
        pairs = lined[:].rearrange("p j (v e) -> p j v e", e=2)
        small = [keep.tile([P, PACK, w], F32, name="small%d" % c) for c in range(2)]
        large = [keep.tile([P, PACK, w], F32, name="large%d" % c) for c in range(2)]
        sig = [keep.tile([P, PACK, w], F32, name="sig%d" % c) for c in range(2)]
        z_rows = [keep.tile([P, PACK, w], BF16, name="z_rows%d" % c) for c in range(2)]
        z_bf = [keep.tile([P, w, PACK], BF16, name="z_bf%d" % c, align_bytes=64) for c in range(2)]
        z_codes = [keep.tile([P, w], U32, name="z_codes%d" % c, align_bytes=64) for c in range(2)]
        z_scale = [keep.tile([P, w], U8, name="z_scale%d" % c, align_bytes=64) for c in range(2)]
        res = [keep.tile([P, N // P, w], F32, name="res%d" % c) for c in range(2)]

        def fetch(c, j):
            nc.vector.tensor_copy(lined[:, j, :], y[j][:].indirect(order_sb[:, c * w // 8 : (c + 1) * w // 8]))

        def smaller(c, h):
            js = slice(2 * h, 2 * h + 2)
            nc.vector.tensor_tensor(small[c][:, js, :], pairs[:, js, :, 0], pairs[:, js, :, 1], ALU.min)
            nc.scalar.activation(sig[c][:, js, :], small[c][:, js, :], ACT.Sigmoid)

        def larger(c, h):
            js = slice(2 * h, 2 * h + 2)
            nc.vector.tensor_tensor(large[c][:, js, :], pairs[:, js, :, 0], pairs[:, js, :, 1], ALU.max)

        def weigh(c, j):
            nc.vector.scalar_tensor_tensor(z_rows[c][:, j, :], large[c][:, j, :], gate[:, j : j + 1], sig[c][:, j, :], ALU.mult, ALU.mult)

        def mix(c, bank, blocks, on_scalar):
            acc = psum.tile([P, 512], F32, name="acc%d" % bank, tag="bank%d" % bank)
            for i, b in enumerate(blocks):
                cols = slice(b * P, (b + 1) * P)
                nc.tensor.matmul_mx(out=acc[:, i * w : (i + 1) * w], lhsT=w1_codes[:, cols].bitcast(FP8X4), lhsT_scale=w1_scale[:, cols],
                                    rhs=z_codes[c][:].bitcast(FP8X4), rhs_scale=z_scale[c][:], start=True, stop=True)
            rows = res[c][:, blocks[0] : blocks[-1] + 1, :]
            if on_scalar:
                nc.scalar.copy(rows.rearrange("p b v -> p (b v)"), acc[:, 0 : len(blocks) * w])
            else:
                nc.vector.tensor_copy(rows.rearrange("p b v -> p (b v)"), acc[:, 0 : len(blocks) * w])

        def store(c, first, last):
            nc.sync.dma_start(out_rows[:, first:last, c * w : (c + 1) * w], res[c][:, first:last, :])

        for j in range(PACK):
            fetch(0, j)
        for h in range(2):
            smaller(0, h)
            larger(0, h)
        group_w1(1)
        fetch(1, 0)
        fetch(1, 1)
        weigh(0, 0)
        weigh(0, 1)
        fetch(1, 2)
        weigh(0, 2)
        weigh(0, 3)
        interleave(True, z_bf[0][:], z_rows[0][:])
        fetch(1, 3)
        quantize(w1_codes[:], w1_scale[:], w1_bf[:])
        smaller(1, 0)
        smaller(1, 1)
        quantize(z_codes[0][:], z_scale[0][:], z_bf[0][:])
        larger(1, 0)
        larger(1, 1)
        mix(0, 0, [0, 1, 2, 3], True)
        store(0, 0, 4)
        for j in range(PACK):
            weigh(1, j)
        interleave(False, z_bf[1][:], z_rows[1][:])
        quantize(z_codes[1][:], z_scale[1][:], z_bf[1][:])
        for b in range(N // P):
            mix(1, 1 + b, [b], b % 2 == 0)
            if b % 2 == 1:
                store(1, b - 1, b + 1)
